import numpy as np
CORES = [0,16,32,48,64,80,96,112,128,144,160,176,192,208,224,240]
N = 16
T, K = 4, 4
ROUTE = [[[10,0,11,2],[1,15,13,6],[5,0,3,9],[2,10,4,6]],[[1,0,9,4],[11,3,7,8],[11,5,0,12],[7,14,9,1]],[[5,6,15,4],[6,12,4,9],[10,5,12,4],[7,13,15,1]],[[12,9,10,3],[9,10,0,2],[11,14,3,1],[15,10,4,13]],[[9,3,5,13],[4,13,7,10],[14,12,2,7],[12,7,6,9]],[[2,11,13,9],[3,14,9,8],[14,7,0,3],[5,10,9,2]],[[10,8,12,9],[12,10,5,11],[6,2,12,9],[15,14,8,11]],[[15,2,11,8],[3,14,2,15],[15,7,0,9],[9,15,2,6]],[[15,4,8,9],[13,14,11,1],[9,1,0,14],[1,2,4,5]],[[7,11,5,8],[5,1,12,3],[3,8,6,1],[15,3,13,4]],[[0,9,14,10],[12,3,13,11],[2,8,12,1],[2,6,5,12]],[[1,9,8,14],[15,8,7,11],[11,10,13,12],[2,1,0,11]],[[3,1,6,11],[13,0,14,10],[3,15,12,14],[15,8,9,7]],[[0,15,10,12],[6,0,15,12],[0,10,11,7],[4,15,10,0]],[[14,6,2,10],[11,6,8,14],[11,12,6,8],[12,0,10,3]],[[9,8,5,1],[15,3,12,6],[15,2,8,10],[6,4,8,9]]]
ZW = 22
def setup_inputs(rng):
    return {"z": rng.standard_normal((N, 128, ZW), dtype=np.float32), "g": rng.random((N, 128, T * K), dtype=np.float32)}
def reference(z, g):
    y = np.zeros((N, 128, T), np.float64)
    fill = [0] * N
    for r in range(N):
        for t in range(T):
            for k, e in enumerate(ROUTE[r][t]):
                y[r][:, t] += g[r][:, t * K + k].astype(np.float64) * z[e][:, fill[e]].astype(np.float64)
                fill[e] += 1
    return {"y": y.astype(z.dtype)}

@@ -1,0 +1,104 @@
+from concourse.bass import DstId, RemoteDMATransfer
+from concourse.mybir import AluOpType
+
+SCRATCH = {
+    "zs": ("sbuf", [128, 22], "float32"),
+    "gs": ("sbuf", [128, 16], "float32"),
+    "land": ("sbuf", [128, 16], "float32"),
+    "prod": ("sbuf", [128, 16], "float32"),
+    "half": ("sbuf", [128, 8], "float32"),
+    "ys": ("sbuf", [128, 4], "float32"),
+}
+SEMAPHORES = ["zl", "gl", "arrived", "sent", "vm", "va", "vb", "stored"]
+
+
+def make_plan(tab):
+    route, n_tok, n_k = tab["ROUTE"], tab["T"], tab["K"]
+    n = len(route)
+    fill = [0] * n
+    blocks = {}
+    for r in range(n):
+        for t in range(n_tok):
+            for k in range(n_k):
+                e = route[r][t][k]
+                if (e, r) not in blocks:
+                    blocks[(e, r)] = (fill[e], [])
+                blocks[(e, r)][1].append((t, k))
+                fill[e] += 1
+    land_at = {}
+    for r in range(n):
+        at = 0
+        for e in range(n):
+            if e != r and (e, r) in blocks:
+                land_at[(e, r)] = at
+                at += len(blocks[(e, r)][1])
+    calls = []
+    incoming = [0] * n
+    for e in range(n):
+        mine = []
+        for width in range(1, n_tok + 1):
+            dsts = [r for r in range(n) if r != e and (e, r) in blocks and len(blocks[(e, r)][1]) == width]
+            for i in range(0, len(dsts), 8):
+                part = dsts[i:i + 8]
+                eng = 8
+                while eng * len(part) > 8:
+                    eng //= 2
+                mine.append([(r, eng) for r in part])
+                for r in part:
+                    incoming[r] += eng
+        calls.append(mine)
+    return blocks, land_at, calls, incoming, fill
+
+
+def rank_program(g, core, T, topo):
+    me = T.rank_of(core)
+    if me is None:
+        return
+    tab = T.tables
+    n_tok, n_k = tab["T"], tab["K"]
+    blocks, land_at, calls, incoming, fill = make_plan(tab)
+    S = T.sem
+
+    g.sync.dma_start(T.zs[:, 0:fill[me]], T.z[:, 0:fill[me]]).then_inc(S.zl, 16)
+    g.scalar.dma_start(T.gs[:], T.g[:]).then_inc(S.gl, 16)
+
+    g.wait_ge(S.zl, 16)
+    left = 0
+    for call in calls[me]:
+        transfers = []
+        first = 0
+        for r, eng in call:
+            col, toks = blocks[(me, r)]
+            w = len(toks)
+            rid, pid = topo.addr(T.cores[r], core)
+            at = land_at[(me, r)]
+            transfers.append(RemoteDMATransfer(
+                dst_ids=[DstId(rid=rid, pnc=pid)], dma_engine_mask=((1 << eng) - 1) << first, remote_sem=S.arrived,
+                src=T.zs[:, col:col + w], dst=T.land[:, at:at + w]))
+            first += eng
+            left += eng
+        g.remote_dma_fused(transfers, local_sem=S.sent)
+
+    v = g.vector
+    v.wait_ge(S.gl, 16)
+    v.wait_ge(S.zl, 16)
+    v.wait_ge(S.arrived, incoming[me])
+    n_mul = 0
+    for e in range(len(T.cores)):
+        if (e, me) not in blocks:
+            continue
+        col, toks = blocks[(e, me)]
+        for i, (t, k) in enumerate(toks):
+            src = T.zs[:, col + i:col + i + 1] if e == me else T.land[:, land_at[(e, me)] + i:land_at[(e, me)] + i + 1]
+            v.tensor_tensor(T.prod[:, k * n_tok + t:k * n_tok + t + 1], T.gs[:, t * n_k + k:t * n_k + k + 1], src,
+                            AluOpType.mult).then_inc(S.vm, 1)
+            n_mul += 1
+    v.wait_ge(S.vm, n_mul)
+    v.tensor_tensor(T.half[:], T.prod[:, 0:8], T.prod[:, 8:16], AluOpType.add).then_inc(S.va, 1)
+    v.wait_ge(S.va, 1)
+    v.tensor_tensor(T.ys[:], T.half[:, 0:4], T.half[:, 4:8], AluOpType.add).then_inc(S.vb, 1)
+
+    g.sync.wait_ge(S.vb, 1)
+    g.sync.dma_start(T.y[:], T.ys[:]).then_inc(S.stored, 16)
+    g.sync.wait_ge(S.stored, 16)
+    g.wait_ge(S.sent, left)

@@ -9,22 +9,98 @@ SCRATCH = {
     "half": ("sbuf", [128, 8], "float32"),
     "ys": ("sbuf", [128, 4], "float32"),
 }
-SEMAPHORES = ["zl", "gl", "arrived", "sent", "vm", "va", "vb", "stored"]
+SEMAPHORES = ["zl", "gl", "handed", "near", "far", "sent", "vm", "va", "vb", "stored"]
+
+MAX_HELPERS = 4
+MAX_BLOCKS = 2
 
 
-def make_plan(tab):
+def find_blocks(tab):
     route, n_tok, n_k = tab["ROUTE"], tab["T"], tab["K"]
-    n = len(route)
-    fill = [0] * n
+    fill = [0] * len(route)
     blocks = {}
-    for r in range(n):
+    for r in range(len(route)):
         for t in range(n_tok):
             for k in range(n_k):
                 e = route[r][t][k]
                 if (e, r) not in blocks:
                     blocks[(e, r)] = (fill[e], [])
-                blocks[(e, r)][1].append((t, k))
+                blocks[(e, r)][1].append(t * n_k + k)
                 fill[e] += 1
+    return blocks, fill
+
+
+def choose_dies(blocks, n):
+    width = {p: len(b[1]) for p, b in blocks.items()}
+    away = [[r for r in range(n) if r != e and (e, r) in blocks] for e in range(n)]
+    side = {(e, r): 1 for e in range(n) for r in away[e]}
+    out = [[0, sum(width[(e, r)] for r in away[e])] for e in range(n)]
+    inn = [[0, sum(width[(e, r)] for e in range(n) if r in away[e])] for r in range(n)]
+
+    def groups(e):
+        gs = []
+        for r in away[e]:
+            if side[(e, r)] == 0:
+                last = gs[-1][-1] if gs else None
+                if gs and len(gs[-1]) < MAX_BLOCKS and blocks[(e, last)][0] + width[(e, last)] == blocks[(e, r)][0]:
+                    gs[-1].append(r)
+                else:
+                    gs.append([r])
+        return gs
+
+    def flip(e, rs):
+        for r in rs:
+            d, w = side[(e, r)], width[(e, r)]
+            out[e][d] -= w
+            inn[r][d] -= w
+            out[e][1 - d] += w
+            inn[r][1 - d] += w
+            side[(e, r)] = 1 - d
+
+    def uneven(e, rs):
+        return ((out[e][0] - out[e][1]) ** 2 + sum((inn[r][0] - inn[r][1]) ** 2 for r in rs),
+                sum(side[(e, r)] for r in away[e]))
+
+    def subsets(rs, size):
+        if size == 0:
+            return [[]]
+        return [[r] + rest for i, r in enumerate(rs) for rest in subsets(rs[i + 1:], size - 1)]
+
+    better = True
+    while better:
+        better = False
+        for e in range(n):
+            for size in (1, 2, 3):
+                for rs in subsets(away[e], size):
+                    before = uneven(e, rs)
+                    flip(e, rs)
+                    if uneven(e, rs) < before and len(groups(e)) <= MAX_HELPERS:
+                        better = True
+                    else:
+                        flip(e, rs)
+    far = [groups(e) for e in range(n)]
+    near = [[r for r in away[e] if side[(e, r)] == 1] for e in range(n)]
+    return near, far
+
+
+def into_calls(items, engines):
+    calls = []
+    for width in sorted(set(it[0] for it in items), reverse=True):
+        same = [it for it in items if it[0] == width]
+        while same:
+            size = engines
+            while size > len(same):
+                size //= 2
+            each = engines // size
+            calls.append([(it, j * each, each) for j, it in enumerate(same[:size])])
+            same = same[size:]
+    return calls
+
+
+def make_plan(tab):
+    n = len(tab["ROUTE"])
+    blocks, fill = find_blocks(tab)
+    near, far = choose_dies(blocks, n)
     land_at = {}
     for r in range(n):
         at = 0
@@ -32,71 +108,129 @@ def make_plan(tab):
             if e != r and (e, r) in blocks:
                 land_at[(e, r)] = at
                 at += len(blocks[(e, r)][1])
-    calls = []
-    incoming = [0] * n
+    near_calls = [into_calls([(len(blocks[(e, r)][1]), r) for r in near[e]], 8) for e in range(n)]
+    far_calls = [[into_calls([(len(blocks[(e, r)][1]), r) for r in grp], 8) for grp in far[e]] for e in range(n)]
+    hand_calls = []
     for e in range(n):
-        mine = []
-        for width in range(1, n_tok + 1):
-            dsts = [r for r in range(n) if r != e and (e, r) in blocks and len(blocks[(e, r)][1]) == width]
-            for i in range(0, len(dsts), 8):
-                part = dsts[i:i + 8]
-                eng = 8
-                while eng * len(part) > 8:
-                    eng //= 2
-                mine.append([(r, eng) for r in part])
-                for r in part:
-                    incoming[r] += eng
-        calls.append(mine)
-    return blocks, land_at, calls, incoming, fill
+        items = []
+        for h, grp in enumerate(far[e]):
+            items.append((sum(len(blocks[(e, r)][1]) for r in grp), h, blocks[(e, grp[0])][0]))
+        hand_calls.append(into_calls(items, 16))
+    near_in, far_in = [0] * n, [0] * n
+    for e in range(n):
+        for call in near_calls[e]:
+            for it, first, each in call:
+                near_in[it[1]] += each
+        for calls in far_calls[e]:
+            for call in calls:
+                for it, first, each in call:
+                    far_in[it[1]] += each
+    return {"blocks": blocks, "fill": fill, "near": near, "far": far, "land_at": land_at, "near_calls": near_calls,
+            "far_calls": far_calls, "hand_calls": hand_calls, "near_in": near_in, "far_in": far_in}
+
+
+PLANS = {}
+
+
+def send_blocks(g, core, T, topo, plan, e, calls, sem):
+    left = 0
+    for call in calls:
+        transfers = []
+        for (w, r), first, each in call:
+            col = plan["blocks"][(e, r)][0]
+            at = plan["land_at"][(e, r)]
+            rid, pid = topo.addr(T.cores[r], core)
+            transfers.append(RemoteDMATransfer(
+                dst_ids=[DstId(rid=rid, pnc=pid)], dma_engine_mask=((1 << each) - 1) << first, remote_sem=sem,
+                src=T.zs[:, col:col + w], dst=T.land[:, at:at + w]))
+            left += each
+        g.remote_dma_fused(transfers, local_sem=T.sem.sent)
+    return left
+
+
+def runs(cols):
+    out = []
+    i = 0
+    while i < len(cols):
+        if i + 1 == len(cols):
+            out.append((cols[i], 1, 1))
+            break
+        step = cols[i + 1] - cols[i]
+        j = i + 1
+        while j + 1 < len(cols) and cols[j + 1] - cols[j] == step:
+            j += 1
+        out.append((cols[i], step, j - i + 1))
+        i = j + 1
+    return out
 
 
 def rank_program(g, core, T, topo):
-    me = T.rank_of(core)
-    if me is None:
+    chip0 = core - core % 8
+    owners = [c for c in range(chip0, chip0 + 8) if T.rank_of(c) is not None]
+    if not owners:
         return
-    tab = T.tables
-    n_tok, n_k = tab["T"], tab["K"]
-    blocks, land_at, calls, incoming, fill = make_plan(tab)
+    owner = owners[0]
+    helpers = [c for c in range(chip0, chip0 + 8) if topo.die(c) != topo.die(owner)][:MAX_HELPERS]
+    if core != owner and core not in helpers:
+        return
+    if "plan" not in PLANS:
+        PLANS["plan"] = make_plan(T.tables)
+    plan = PLANS["plan"]
     S = T.sem
+    me = T.rank_of(owner)
 
-    g.sync.dma_start(T.zs[:, 0:fill[me]], T.z[:, 0:fill[me]]).then_inc(S.zl, 16)
+    if core != owner:
+        h = helpers.index(core)
+        if h >= len(plan["far"][me]):
+            return
+        got = sum(each for call in plan["hand_calls"][me] for it, first, each in call if it[1] == h)
+        g.wait_ge(S.handed, got)
+        left = send_blocks(g, core, T, topo, plan, me, plan["far_calls"][me][h], S.far)
+        g.wait_ge(S.sent, left)
+        return
+
+    blocks, land_at = plan["blocks"], plan["land_at"]
+    nz = plan["fill"][me]
+    g.sync.dma_start(T.zs[:, 0:nz], T.z[:, 0:nz]).then_inc(S.zl, 16)
     g.scalar.dma_start(T.gs[:], T.g[:]).then_inc(S.gl, 16)
 
     g.wait_ge(S.zl, 16)
     left = 0
-    for call in calls[me]:
+    for call in plan["hand_calls"][me]:
         transfers = []
-        first = 0
-        for r, eng in call:
-            col, toks = blocks[(me, r)]
-            w = len(toks)
-            rid, pid = topo.addr(T.cores[r], core)
-            at = land_at[(me, r)]
+        for (w, h, col), first, each in call:
+            rid, pid = topo.addr(helpers[h], core)
             transfers.append(RemoteDMATransfer(
-                dst_ids=[DstId(rid=rid, pnc=pid)], dma_engine_mask=((1 << eng) - 1) << first, remote_sem=S.arrived,
-                src=T.zs[:, col:col + w], dst=T.land[:, at:at + w]))
-            first += eng
-            left += eng
+                dst_ids=[DstId(rid=rid, pnc=pid)], dma_engine_mask=((1 << each) - 1) << first, remote_sem=S.handed,
+                src=T.zs[:, col:col + w], dst=T.zs[:, col:col + w]))
+            left += each
         g.remote_dma_fused(transfers, local_sem=S.sent)
+    left += send_blocks(g, core, T, topo, plan, me, plan["near_calls"][me], S.near)
 
     v = g.vector
+    n = len(T.cores)
+    n_mul = 0
     v.wait_ge(S.gl, 16)
     v.wait_ge(S.zl, 16)
-    v.wait_ge(S.arrived, incoming[me])
-    n_mul = 0
-    for e in range(len(T.cores)):
-        if (e, me) not in blocks:
-            continue
-        col, toks = blocks[(e, me)]
-        for i, (t, k) in enumerate(toks):
-            src = T.zs[:, col + i:col + i + 1] if e == me else T.land[:, land_at[(e, me)] + i:land_at[(e, me)] + i + 1]
-            v.tensor_tensor(T.prod[:, k * n_tok + t:k * n_tok + t + 1], T.gs[:, t * n_k + k:t * n_k + k + 1], src,
-                            AluOpType.mult).then_inc(S.vm, 1)
-            n_mul += 1
+    kinds = [([me] if (me, me) in blocks else [], None, 0),
+             ([e for e in range(n) if me in plan["near"][e]], S.near, plan["near_in"][me]),
+             ([e for e in range(n) if any(me in grp for grp in plan["far"][e])], S.far, plan["far_in"][me])]
+    for experts, sem, count in kinds:
+        if count:
+            v.wait_ge(sem, count)
+        for e in experts:
+            col, cols = blocks[(e, me)]
+            buf, at = (T.zs, col) if e == me else (T.land, land_at[(e, me)])
+            for first, step, cnt in runs(cols):
+                stop = first + step * (cnt - 1) + 1
+                v.tensor_tensor(T.prod[:, first:stop:step], T.gs[:, first:stop:step], buf[:, at:at + cnt],
+                                AluOpType.mult).then_inc(S.vm, 1)
+                at += cnt
+                n_mul += 1
     v.wait_ge(S.vm, n_mul)
-    v.tensor_tensor(T.half[:], T.prod[:, 0:8], T.prod[:, 8:16], AluOpType.add).then_inc(S.va, 1)
+    v.tensor_tensor(T.half[:], T.prod[:, 0:16:2], T.prod[:, 1:16:2], AluOpType.add).then_inc(S.va, 1)
     v.wait_ge(S.va, 1)
-    v.tensor_tensor(T.ys[:], T.half[:, 0:4], T.half[:, 4:8], AluOpType.add).then_inc(S.vb, 1)
+    v.tensor_tensor(T.ys[:], T.half[:, 0:8:2], T.half[:, 1:8:2], AluOpType.add).then_inc(S.vb, 1)
 
     g.sync.wait_ge(S.vb, 1)
     g.sync.dma_start(T.y[:], T.ys[:]).then_inc(S.stored, 16)

from concourse.bass import DstId, RemoteDMATransfer
from concourse.mybir import AluOpType

SCRATCH = {
    "zs": ("sbuf", [128, 22], "float32"),
    "gs": ("sbuf", [128, 16], "float32"),
    "land": ("sbuf", [128, 16], "float32"),
    "prod": ("sbuf", [128, 16], "float32"),
    "half": ("sbuf", [128, 8], "float32"),
    "ys": ("sbuf", [128, 4], "float32"),
}
SEMAPHORES = ["zl", "gl", "handed", "near", "far", "sent", "vm", "va", "vb", "stored"]

MAX_HELPERS = 4
MAX_BLOCKS = 2


def find_blocks(tab):
    route, n_tok, n_k = tab["ROUTE"], tab["T"], tab["K"]
    fill = [0] * len(route)
    blocks = {}
    for r in range(len(route)):
        for t in range(n_tok):
            for k in range(n_k):
                e = route[r][t][k]
                if (e, r) not in blocks:
                    blocks[(e, r)] = (fill[e], [])
                blocks[(e, r)][1].append(t * n_k + k)
                fill[e] += 1
    return blocks, fill


def choose_dies(blocks, n):
    width = {p: len(b[1]) for p, b in blocks.items()}
    away = [[r for r in range(n) if r != e and (e, r) in blocks] for e in range(n)]
    side = {(e, r): 1 for e in range(n) for r in away[e]}
    out = [[0, sum(width[(e, r)] for r in away[e])] for e in range(n)]
    inn = [[0, sum(width[(e, r)] for e in range(n) if r in away[e])] for r in range(n)]

    def groups(e):
        gs = []
        for r in away[e]:
            if side[(e, r)] == 0:
                last = gs[-1][-1] if gs else None
                if gs and len(gs[-1]) < MAX_BLOCKS and blocks[(e, last)][0] + width[(e, last)] == blocks[(e, r)][0]:
                    gs[-1].append(r)
                else:
                    gs.append([r])
        return gs

    def flip(e, rs):
        for r in rs:
            d, w = side[(e, r)], width[(e, r)]
            out[e][d] -= w
            inn[r][d] -= w
            out[e][1 - d] += w
            inn[r][1 - d] += w
            side[(e, r)] = 1 - d

    def uneven(e, rs):
        return ((out[e][0] - out[e][1]) ** 2 + sum((inn[r][0] - inn[r][1]) ** 2 for r in rs),
                sum(side[(e, r)] for r in away[e]))

    def subsets(rs, size):
        if size == 0:
            return [[]]
        return [[r] + rest for i, r in enumerate(rs) for rest in subsets(rs[i + 1:], size - 1)]

    better = True
    while better:
        better = False
        for e in range(n):
            for size in (1, 2, 3):
                for rs in subsets(away[e], size):
                    before = uneven(e, rs)
                    flip(e, rs)
                    if uneven(e, rs) < before and len(groups(e)) <= MAX_HELPERS:
                        better = True
                    else:
                        flip(e, rs)
    far = [groups(e) for e in range(n)]
    near = [[r for r in away[e] if side[(e, r)] == 1] for e in range(n)]
    return near, far


def into_calls(items, engines):
    calls = []
    for width in sorted(set(it[0] for it in items), reverse=True):
        same = [it for it in items if it[0] == width]
        while same:
            size = engines
            while size > len(same):
                size //= 2
            each = engines // size
            calls.append([(it, j * each, each) for j, it in enumerate(same[:size])])
            same = same[size:]
    return calls


def make_plan(tab):
    n = len(tab["ROUTE"])
    blocks, fill = find_blocks(tab)
    near, far = choose_dies(blocks, n)
    land_at = {}
    for r in range(n):
        at = 0
        for e in range(n):
            if e != r and (e, r) in blocks:
                land_at[(e, r)] = at
                at += len(blocks[(e, r)][1])
    near_calls = [into_calls([(len(blocks[(e, r)][1]), r) for r in near[e]], 8) for e in range(n)]
    far_calls = [[into_calls([(len(blocks[(e, r)][1]), r) for r in grp], 8) for grp in far[e]] for e in range(n)]
    hand_calls = []
    for e in range(n):
        items = []
        for h, grp in enumerate(far[e]):
            items.append((sum(len(blocks[(e, r)][1]) for r in grp), h, blocks[(e, grp[0])][0]))
        hand_calls.append(into_calls(items, 16))
    near_in, far_in = [0] * n, [0] * n
    for e in range(n):
        for call in near_calls[e]:
            for it, first, each in call:
                near_in[it[1]] += each
        for calls in far_calls[e]:
            for call in calls:
                for it, first, each in call:
                    far_in[it[1]] += each
    return {"blocks": blocks, "fill": fill, "near": near, "far": far, "land_at": land_at, "near_calls": near_calls,
            "far_calls": far_calls, "hand_calls": hand_calls, "near_in": near_in, "far_in": far_in}


PLANS = {}


def send_blocks(g, core, T, topo, plan, e, calls, sem):
    left = 0
    for call in calls:
        transfers = []
        for (w, r), first, each in call:
            col = plan["blocks"][(e, r)][0]
            at = plan["land_at"][(e, r)]
            rid, pid = topo.addr(T.cores[r], core)
            transfers.append(RemoteDMATransfer(
                dst_ids=[DstId(rid=rid, pnc=pid)], dma_engine_mask=((1 << each) - 1) << first, remote_sem=sem,
                src=T.zs[:, col:col + w], dst=T.land[:, at:at + w]))
            left += each
        g.remote_dma_fused(transfers, local_sem=T.sem.sent)
    return left


def runs(cols):
    out = []
    i = 0
    while i < len(cols):
        if i + 1 == len(cols):
            out.append((cols[i], 1, 1))
            break
        step = cols[i + 1] - cols[i]
        j = i + 1
        while j + 1 < len(cols) and cols[j + 1] - cols[j] == step:
            j += 1
        out.append((cols[i], step, j - i + 1))
        i = j + 1
    return out


def rank_program(g, core, T, topo):
    chip0 = core - core % 8
    owners = [c for c in range(chip0, chip0 + 8) if T.rank_of(c) is not None]
    if not owners:
        return
    owner = owners[0]
    helpers = [c for c in range(chip0, chip0 + 8) if topo.die(c) != topo.die(owner)][:MAX_HELPERS]
    if core != owner and core not in helpers:
        return
    if "plan" not in PLANS:
        PLANS["plan"] = make_plan(T.tables)
    plan = PLANS["plan"]
    S = T.sem
    me = T.rank_of(owner)

    if core != owner:
        h = helpers.index(core)
        if h >= len(plan["far"][me]):
            return
        got = sum(each for call in plan["hand_calls"][me] for it, first, each in call if it[1] == h)
        g.wait_ge(S.handed, got)
        left = send_blocks(g, core, T, topo, plan, me, plan["far_calls"][me][h], S.far)
        g.wait_ge(S.sent, left)
        return

    blocks, land_at = plan["blocks"], plan["land_at"]
    nz = plan["fill"][me]
    g.sync.dma_start(T.zs[:, 0:nz], T.z[:, 0:nz]).then_inc(S.zl, 16)
    g.scalar.dma_start(T.gs[:], T.g[:]).then_inc(S.gl, 16)

    g.wait_ge(S.zl, 16)
    left = 0
    for call in plan["hand_calls"][me]:
        transfers = []
        for (w, h, col), first, each in call:
            rid, pid = topo.addr(helpers[h], core)
            transfers.append(RemoteDMATransfer(
                dst_ids=[DstId(rid=rid, pnc=pid)], dma_engine_mask=((1 << each) - 1) << first, remote_sem=S.handed,
                src=T.zs[:, col:col + w], dst=T.zs[:, col:col + w]))
            left += each
        g.remote_dma_fused(transfers, local_sem=S.sent)
    left += send_blocks(g, core, T, topo, plan, me, plan["near_calls"][me], S.near)

    v = g.vector
    n = len(T.cores)
    n_mul = 0
    v.wait_ge(S.gl, 16)
    v.wait_ge(S.zl, 16)
    kinds = [([me] if (me, me) in blocks else [], None, 0),
             ([e for e in range(n) if me in plan["near"][e]], S.near, plan["near_in"][me]),
             ([e for e in range(n) if any(me in grp for grp in plan["far"][e])], S.far, plan["far_in"][me])]
    for experts, sem, count in kinds:
        if count:
            v.wait_ge(sem, count)
        for e in experts:
            col, cols = blocks[(e, me)]
            buf, at = (T.zs, col) if e == me else (T.land, land_at[(e, me)])
            for first, step, cnt in runs(cols):
                stop = first + step * (cnt - 1) + 1
                v.tensor_tensor(T.prod[:, first:stop:step], T.gs[:, first:stop:step], buf[:, at:at + cnt],
                                AluOpType.mult).then_inc(S.vm, 1)
                at += cnt
                n_mul += 1
    v.wait_ge(S.vm, n_mul)
    v.tensor_tensor(T.half[:], T.prod[:, 0:16:2], T.prod[:, 1:16:2], AluOpType.add).then_inc(S.va, 1)
    v.wait_ge(S.va, 1)
    v.tensor_tensor(T.ys[:], T.half[:, 0:8:2], T.half[:, 1:8:2], AluOpType.add).then_inc(S.vb, 1)

    g.sync.wait_ge(S.vb, 1)
    g.sync.dma_start(T.y[:], T.ys[:]).then_inc(S.stored, 16)
    g.sync.wait_ge(S.stored, 16)
    g.wait_ge(S.sent, left)
